import numpy as np
import ml_dtypes


def mxq(x, axis, fmt="e4m3"):
    dtype, down = {"e4m3": (ml_dtypes.float8_e4m3fn, 7), "e5m2": (ml_dtypes.float8_e5m2, 14)}[fmt]
    v = np.moveaxis(np.asarray(x, np.float32).astype(ml_dtypes.bfloat16).astype(np.float64), axis, -1)
    blocks = v.reshape(v.shape[:-1] + (-1, 32))
    amax = np.abs(blocks).max(-1, keepdims=True)
    byte = np.maximum(np.where(amax > 0, np.frexp(amax)[1] - 1 + 127, 0) - down, 1)
    scale = np.exp2(byte - 127.0)
    codes = (blocks / scale).astype(np.float32).astype(dtype).astype(np.float64)
    return np.moveaxis((codes * scale).reshape(v.shape), -1, axis)


WIDE = False


def mx_kscale(k):
    if not WIDE:
        return np.ones(k)
    levels = np.array([10, -10, 5, -5, 0])
    if k % 512:
        return np.exp2(np.random.permutation(np.resize(levels, k // 32))).repeat(32)
    a = np.empty((k // 512, 16))
    for p in range(k // 512):
        a[p, :8] = np.random.permutation(np.resize(levels, 8))
        for g in range(8):
            far = levels[np.abs(levels - a[p, g]) >= 10]
            a[p, g + 8] = far[np.random.randint(len(far))]
    return np.exp2(a.ravel()).repeat(32)


BF16 = ml_dtypes.bfloat16


def bf(x):
    return np.asarray(x, np.float32).astype(BF16)


def f64(x):
    return np.asarray(x).astype(np.float64)


E2M1 = np.array([0.0, 0.5, 1.0, 1.5, 2.0, 3.0, 4.0, 6.0, -0.0, -0.5, -1.0, -1.5, -2.0, -3.0, -4.0, -6.0])


def pack_weight(w, fmt):
    k, n = w.shape
    w = f64(bf(w)).reshape(k // 32, 32, n)
    amax = np.abs(w).max(1)
    if fmt == "e4m3":
        byte = np.frexp(amax)[1] - 1 + 127 - 7
    else:
        mant, ex = np.frexp(amax / 6.0)
        byte = np.where(mant > 0.5, ex, ex - 1) + 127
    byte = np.clip(np.where(amax > 0, byte, 1), 1, 254)
    scaled = (w * np.exp2(127.0 - byte)[:, None, :]).reshape(k, n).astype(np.float32)
    by_word = np.ascontiguousarray(scaled.reshape(k // 512, 128, 4, n).transpose(0, 1, 3, 2))
    if fmt == "e4m3":
        words = by_word.astype(ml_dtypes.float8_e4m3fn).view(np.uint8)
    else:
        c = by_word.astype(ml_dtypes.float4_e2m1fn).view(np.uint8) & 0xF
        words = c[..., 0::2] | (c[..., 1::2] << 4)
    return np.ascontiguousarray(words), np.ascontiguousarray(byte.astype(np.uint8).reshape(k // 512, 16, n))


def unpack_weight(words, scales, fmt):
    g, p, n, _ = words.shape
    if fmt == "e4m3":
        vals = np.ascontiguousarray(words).view(ml_dtypes.float8_e4m3fn).astype(np.float64)
    else:
        nib = np.empty((g, p, n, 4), np.uint8)
        nib[..., 0::2] = words & 0xF
        nib[..., 1::2] = words >> 4
        vals = E2M1[nib]
    vals = vals * np.repeat(np.exp2(scales.astype(np.float64) - 127.0), 8, axis=1)[..., None]
    return vals.transpose(0, 1, 3, 2).reshape(g * 512, n)

def planes(Y):
    n, m = Y.shape
    b = f64(bf(Y)).reshape(n // 32, 32, m)
    amax = np.abs(b).max(1)
    byte = np.clip(np.where(amax > 0, np.frexp(amax)[1] - 1 + 127 - 7, 1), 1, 254)
    codes = (b * np.exp2(127.0 - byte)[:, None, :]).reshape(n, m).astype(np.float32).astype(ml_dtypes.float8_e4m3fn).view(np.uint8)
    words = codes.reshape(n // 512, 128, 4, m).transpose(0, 1, 3, 2)
    return np.ascontiguousarray(words), np.ascontiguousarray(byte.astype(np.uint8).reshape(n // 512, 16, m))


M, P, S = 1024, 1024, 1024

MU = 0.4


def coulomb_stress(slip, kt_words, kt_scales, kn_words, kn_scales, tau0):
    slip_q = mxq(f64(slip), 1, "e4m3")
    st = slip_q @ unpack_weight(kt_words, kt_scales, "e4m3")
    sn = slip_q @ unpack_weight(kn_words, kn_scales, "e4m3")
    return f64(tau0)[None, :] - st + MU * sn


def slip_rate(r):
    return 0.5 * (np.exp(r) - np.exp(-r))


def setup_inputs():
    s, t = mx_kscale(P), mx_kscale(P)
    slip = bf(np.random.standard_normal((M, P)) * s)
    kt_words, kt_scales = pack_weight(np.random.standard_normal((P, P)) * (0.7 / np.sqrt(P)) / s[:, None], "e4m3")
    kn_words, kn_scales = pack_weight(np.random.standard_normal((P, P)) * (0.7 / np.sqrt(P)) / s[:, None], "e4m3")
    tau0 = bf(0.5 * np.random.standard_normal(P))
    a = bf(np.random.uniform(1.0, 2.0, P))
    area = bf((1.0 + 0.1 * np.random.standard_normal(P)) * t)
    g_words, g_scales = pack_weight(np.random.standard_normal((P, S)) * (1.0 / np.sqrt(P)) / t[:, None], "e4m3")
    return {
        "slip": slip,
        "kt_words": kt_words,
        "kt_scales": kt_scales,
        "kn_words": kn_words,
        "kn_scales": kn_scales,
        "tau0": tau0,
        "a": a,
        "area": area,
        "g_words": g_words,
        "g_scales": g_scales,
    }


def core(slip, kt_words, kt_scales, kn_words, kn_scales, tau0, a, area, g_words, g_scales):
    cfs = coulomb_stress(slip, kt_words, kt_scales, kn_words, kn_scales, tau0)
    r = cfs / f64(a)[None, :]
    vel = slip_rate(r)
    p = vel * f64(area)[None, :]
    return mxq(p, 1, "e4m3") @ unpack_weight(g_words, g_scales, "e4m3")


def reference(slip, kt_words, kt_scales, kn_words, kn_scales, tau0, a, area, g_words, g_scales):
    R_out = core(slip, kt_words, kt_scales, kn_words, kn_scales, tau0, a, area, g_words, g_scales)
    words, scales = planes(R_out)
    return R_out, words, scales

from contextlib import ExitStack

import concourse.mybir as mybir
from concourse.masks import make_identity

M = 1024
K = 1024
S = 1024
FLOPS = 2 * M * K * (K + K + S)
BYTES = 2 * M * K + 3 * (K * K + K * K // 32) + 3 * 2 * K + 4 * M * S + M * S + M * S // 32

F32 = mybir.dt.float32
BF16 = mybir.dt.bfloat16
I32 = mybir.dt.int32
U32 = mybir.dt.uint32
U8 = mybir.dt.uint8
FP8X4 = mybir.dt.float8_e4m3fn_x4
ALU = mybir.AluOpType
ACT = mybir.ActivationFunctionType

P = 128
MU = 0.4
LEAD = 2
TINY = 1e-18

A_DRAIN = {(0, 0): "v", (0, 1): "v", (1, 0): "v", (1, 1): "s", (2, 0): "s", (2, 1): "s", (3, 0): "v", (3, 1): "s"}
B_DRAIN = {(0, 0): "v", (0, 1): "s", (1, 0): "s", (1, 1): "s", (2, 0): "s", (2, 1): "s", (3, 0): "v", (3, 1): "s"}


def tile_ratestrengtheningafterslipsurfacevelocit_x2_kernel(
    tc, slip, kt_words, kt_scales, kn_words, kn_scales, tau0, a, area, g_words, g_scales, out_0, out_1, out_2
):
    nc = tc.nc
    with ExitStack() as ctx:
        ctx.enter_context(tc.manual_schedule())
        keep = ctx.enter_context(tc.tile_pool(name="keep", bufs=1))
        work = ctx.enter_context(tc.tile_pool(name="work", bufs=2))
        psum = ctx.enter_context(tc.psum_pool(name="psum", bufs=2))

        def kept(shape, dt, name):
            return keep.tile(shape, dt, name=name, align_bytes=64)

        slip_raw = [[kept([P, 2, K], BF16, f"slip_raw{m}{c}") for c in range(2)] for m in range(2)]
        raw_w = {(w, h): kept([P, 2, 512], I32, f"raw_{w}{h}") for w in "nt" for h in range(2)}
        prm_w = {(w, h): kept([P, 2, 512], I32, f"prm_{w}{h}") for w in "nt" for h in range(2)}
        raw_s = kept([P, K], U8, "raw_s")
        prm_s = [kept([P, 512], U8, f"prm_s{h}") for h in range(2)]
        g_w = [kept([P, 2, 512], I32, f"g_w{s}") for s in range(2)]
        g_s = kept([P, S], U8, "g_s")
        slip_c = [kept([P, 2, 512], U32, f"slip_c{m}") for m in range(2)]
        slip_s = [kept([P, 2, 512], U8, f"slip_s{m}") for m in range(2)]
        p_c = [[kept([P, 512], U32, f"p_c{m}{h}") for h in range(2)] for m in range(2)]
        p_s = [[kept([P, 512], U8, f"p_s{m}{h}") for h in range(2)] for m in range(2)]
        out_f = [kept([P, 4, S], F32, f"out_f{m}") for m in range(2)]
        out_b = [[kept([P, 512, 4], BF16, f"out_b{m}{s}") for s in range(2)] for m in range(2)]
        out_c = [kept([P, S], U32, f"out_c{m}") for m in range(2)]
        out_s = [kept([P, S], U8, f"out_s{m}") for m in range(2)]
        ident = kept([P, P], F32, "ident")
        vec = {n: kept([P, 8], BF16, "vec_" + n) for n in ("a", "tau", "area")}
        small = {n: kept([P, 8], F32, "small_" + n) for n in ("ra", "hs", "hm", "h", "rh", "sra", "c1", "b1", "c", "l1", "e", "t", "l")}

        def load_slip(m, c):
            rows = slip[512 * m : 512 * (m + 1), :].rearrange("(q t) k -> q t k", t=4)
            nc.sync.dma_start(out=slip_raw[m][c][:], in_=rows[:, 2 * c : 2 * c + 2, :])

        def load_words(dst, words, c):
            src = words.rearrange("g p n t -> p g (n t)").bitcast(I32)
            nc.sync.dma_start(out=dst[:], in_=src[:, :, 512 * c : 512 * (c + 1)])

        def load_scales(q, dst, row, scales, n, queue):
            queue.dma_start(
                out=dst[32 * q + row : 32 * q + row + 8, :].bitcast(I32),
                in_=scales[:, 4 * q : 4 * q + 4, :].bitcast(I32),
            )

        nc.vector.memset(raw_s[:].bitcast(I32), 0)
        nc.vector.memset(g_s[:].bitcast(I32), 0)
        make_identity(nc, ident[:])
        for n, src in (("area", area), ("a", a), ("tau", tau0)):
            nc.scalar.dma_start(
                out=vec[n][:].rearrange("p (h t) -> p h t", t=4),
                in_=src.rearrange("(h p t) -> p h t", h=2, t=4),
            )
        load_slip(0, 0)
        load_words(raw_w["n", 0], kn_words, 0)
        for i in range(8):
            if i == 5:
                load_words(raw_w["t", 0], kt_words, 0)
            load_scales(i % 4, raw_s, 8 - 8 * (i // 4), (kn_scales, kt_scales)[i // 4], K, nc.sync)
        load_slip(0, 1)
        load_words(raw_w["n", 1], kn_words, 1)
        load_words(raw_w["t", 1], kt_words, 1)
        load_slip(1, 0)
        load_slip(1, 1)
        for q in range(4):
            load_scales(q, g_s, 0, g_scales, S, nc.sync)
        for s in range(2):
            load_words(g_w[s], g_words, s)

        v = {n: t[:] for n, t in small.items()}
        nc.vector.tensor_scalar(out=v["hs"], in0=vec["area"][:], scalar1=0.0, scalar2=0.5, op0=ALU.is_ge, op1=ALU.subtract)
        nc.vector.reciprocal(out=v["ra"], in_=vec["a"][:])
        nc.vector.tensor_tensor(out=v["hm"], in0=v["hs"], in1=vec["area"][:], op=ALU.mult)
        nc.vector.scalar_tensor_tensor(out=v["sra"], in0=v["hs"], scalar=2.0, in1=v["ra"], op0=ALU.mult, op1=ALU.mult)
        nc.vector.tensor_scalar_max(out=v["h"], in0=v["hm"], scalar1=TINY)
        nc.vector.tensor_scalar_mul(out=v["c1"], in0=v["sra"], scalar1=MU)
        nc.vector.tensor_tensor(out=v["b1"], in0=v["sra"], in1=vec["tau"][:], op=ALU.mult)
        nc.vector.tensor_scalar_mul(out=v["c"], in0=v["sra"], scalar1=-1.0)
        nc.vector.reciprocal(out=v["rh"], in_=v["h"])
        nc.scalar.activation(out=v["l1"], in_=v["h"], func=ACT.Ln)

        def finish_l():
            nc.scalar.activation(out=v["e"], in_=v["l1"], func=ACT.Exp)
            nc.vector.tensor_tensor(out=v["t"], in0=v["e"], in1=v["rh"], op=ALU.mult)
            nc.vector.scalar_tensor_tensor(out=v["l"], in0=v["l1"], scalar=1.0, in1=v["t"], op0=ALU.add, op1=ALU.subtract)

        slip_t = {}

        turn_bank = {}

        def turn(m, c, g):
            words = slip_raw[m][c][:].bitcast(F32)
            bank = psum.tile([P, 2, 2, P], F32, tag="s2", name="turn_bank", bufs=4)
            turn_bank[m, c, g] = bank
            for u in range(2):
                for t in range(2):
                    nc.tensor.transpose(bank[:, u, t, :], words[:, t, 256 * g + u : 256 * (g + 1) : 2], ident[:])

        def turn_copy(m, c, g, eng):
            bank = turn_bank[m, c, g]
            dst = work.tile([P, 256, 4], BF16, tag="slip_t", name="slip_t", bufs=4, align_bytes=64)
            slip_t[m, c, g] = dst
            o = dst[:].rearrange("p m j -> p (m j)").bitcast(F32).rearrange("p (m u) -> p m u", u=2)
            i = bank[:].rearrange("p u t q -> p (t q) u")
            if eng == "v":
                nc.vector.tensor_copy(out=o, in_=i)
            else:
                nc.scalar.copy(out=o, in_=i)

        def quant_slip(m, c, g):
            cols = slice(256 * c, 256 * (c + 1))
            nc.vector.quantize_mx(
                out=slip_c[m][:, g, cols].bitcast(FP8X4),
                scales=slip_s[m][:, g, cols],
                in_=slip_t[m, c, g][:].rearrange("p m j -> p (m j)"),
            )

        def permute(w, h):
            nc.vector.tensor_copy(
                out=prm_w[w, h][:].rearrange("p g (t q) -> p g t q", t=4),
                in_=raw_w[w, h][:].rearrange("p g (q t) -> p g t q", t=4),
            )

        def permute_s(h):
            nc.vector.tensor_copy(
                out=prm_s[h][:].rearrange("p (t q) -> p t q", t=4),
                in_=raw_s[:, 512 * h : 512 * (h + 1)].rearrange("p (q t) -> p t q", t=4),
            )

        units = []
        for m, h in ((0, 0), (0, 1), (1, 0), (1, 1)):
            if m == h:
                units += [(m, h, t, 256 * c, 256) for c in range(2) for t in range(4)]
            else:
                units += [(m, h, t, 0, 512) for t in range(4)]
        banks = {}
        xs = {}
        rs = {}
        es = {}

        def mm(i):
            m, h, t, c0, w = units[i]
            cols = slice(c0, c0 + w)
            st_cols = slice(P * t, P * (t + 1))
            for name, row in (("n", 8), ("t", 0)):
                bank = psum.tile([P, 512], F32, tag="s" + name, name="bank_" + name, bufs=2)
                banks[name, i] = bank
                for g in range(2):
                    nc.tensor.matmul_mx(
                        out=bank[:, :w],
                        lhsT=prm_w[name, h][:, g, st_cols].bitcast(FP8X4),
                        lhsT_scale=prm_s[h][row + 4 * g : P, st_cols],
                        rhs=slip_c[m][:, g, cols].bitcast(FP8X4),
                        rhs_scale=slip_s[m][:, g, cols],
                        start=(g == 0),
                        stop=(g == 1),
                    )

        def col(n, i):
            m, h, t, c0, w = units[i]
            j = 4 * h + t
            return small[n][:, j : j + 1]

        def x_step(i):
            w = units[i][4]
            xs[i] = work.tile([P, 512], F32, tag="x", name="x", bufs=4)
            nc.scalar.activation(out=xs[i][:, :w], in_=banks["n", i][:, :w], func=ACT.Identity, scale=col("c1", i), bias=col("b1", i))

        def r_step(i):
            w = units[i][4]
            rs[i] = work.tile([P, 512], F32, tag="r", name="r", bufs=4)
            nc.vector.scalar_tensor_tensor(
                out=rs[i][:, :w], in0=banks["t", i][:, :w], scalar=col("c", i), in1=xs[i][:, :w], op0=ALU.mult, op1=ALU.add
            )

        def e_step(i):
            m, h, t, c0, w = units[i]
            if (m, h) not in es:
                es[m, h] = [work.tile([P, 4, 512], F32, tag=n, name=n, bufs=2) for n in ("ep", "em")]
            for k, sc in ((0, 1.0), (1, -1.0)):
                nc.scalar.activation(out=es[m, h][k][:, t, c0 : c0 + w], in_=rs[i][:, :w], func=ACT.Exp, scale=sc, bias=col("l", i))

        p_b = {}

        def p_piece(m, h, i):
            if (m, h) not in p_b:
                p_b[m, h] = work.tile([P, 512, 4], BF16, tag="p_b", name="p_b", bufs=2, align_bytes=64)
            cols = slice(P * i, P * (i + 1))
            e1, e2 = [e[:, :, cols].rearrange("p t (c i) -> p c t i", i=4) for e in es[m, h]]
            nc.vector.tensor_tensor(
                out=p_b[m, h][:, cols, :].rearrange("p (c i) t -> p c t i", i=4), in0=e1, in1=e2, op=ALU.subtract
            )

        def q_piece(m, h, i):
            cols = slice(P * i, P * (i + 1))
            nc.vector.quantize_mx(
                out=p_c[m][h][:, cols].bitcast(FP8X4),
                scales=p_s[m][h][:, cols],
                in_=p_b[m, h][:, cols, :].rearrange("p m t -> p (m t)"),
            )

        out_bank = {}

        def mm2(m, i, s, tag="s2"):
            bank = psum.tile([P, 512], F32, tag=tag, name="out_bank", bufs=4 if tag == "s2" else 2)
            out_bank[m, i, s] = bank
            cols = slice(P * i, P * (i + 1))
            for h in range(2):
                nc.tensor.matmul_mx(
                    out=bank[:],
                    lhsT=p_c[m][h][:, cols].bitcast(FP8X4),
                    lhsT_scale=p_s[m][h][:, cols],
                    rhs=g_w[s][:, h, :].bitcast(FP8X4),
                    rhs_scale=g_s[4 * h : P, 512 * s : 512 * (s + 1)],
                    start=(h == 0),
                    stop=(h == 1),
                )

        def drain(m, i, s, eng):
            cols = slice(512 * s, 512 * (s + 1))
            o = out_f[m][:, i, cols]
            if eng == "v":
                nc.vector.tensor_copy(out=o, in_=out_bank[m, i, s][:])
            else:
                nc.scalar.copy(out=o, in_=out_bank[m, i, s][:])
            nc.sync.dma_start(out=out_0[512 * m : 512 * (m + 1), :].rearrange("(q t) s -> q t s", t=4)[:, i, cols], in_=o)

        def interleave(m, k, eng):
            cols = slice(256 * k, 256 * (k + 1))
            o = out_b[m][k // 2][:, 256 * (k % 2) : 256 * (k % 2 + 1), :].rearrange("p (c i) t -> p c t i", i=4)
            i = out_f[m][:, :, cols].rearrange("p t (c i) -> p c t i", i=4)
            if eng == "v":
                nc.vector.tensor_copy(out=o, in_=i)
            else:
                nc.gpsimd.tensor_scalar(out=o, in0=i, scalar1=1.0, scalar2=0.0, op0=ALU.mult, op1=ALU.subtract)

        def quant_out(m, k):
            cols = slice(256 * k, 256 * (k + 1))
            nc.vector.quantize_mx(
                out=out_c[m][:, cols].bitcast(FP8X4),
                scales=out_s[m][:, cols],
                in_=out_b[m][k // 2][:, 256 * (k % 2) : 256 * (k % 2 + 1), :].rearrange("p m t -> p (m t)"),
            )

        def store_words(m, s):
            cols = slice(512 * s, 512 * (s + 1))
            nc.sync.dma_start(
                out=out_1[m].rearrange("p m t -> p (m t)").bitcast(I32)[:, cols], in_=out_c[m][:, cols].bitcast(I32)
            )

        def store_scales(m):
            for q in range(4):
                nc.sync.dma_start(
                    out=out_2[m, 4 * q : 4 * q + 4, :].bitcast(I32), in_=out_s[m][32 * q : 32 * q + 4, :].bitcast(I32)
                )

        aux = {}

        def at(slot, fn, *args):
            aux.setdefault(slot, []).append((fn, args))

        for g in range(2):
            at(-1, turn, 0, 1, g)
            at(-1, turn_copy, 0, 1, g, "vs"[g])
            at(0, quant_slip, 0, 1, g)
        at(2, permute, "n", 1)
        at(3, permute, "t", 1)
        at(4, permute_s, 1)
        for i in range(2):
            at(4 + i, p_piece, 0, 0, i)
            at(5 + i, q_piece, 0, 0, i)
            at(8 + i, p_piece, 0, 0, 2 + i)
            at(9 + i, q_piece, 0, 0, 2 + i)
        for c in range(2):
            for g in range(2):
                at(4 + 2 * c, turn, 1, c, g)
                at(5 + 2 * c + g, turn_copy, 1, c, g, "v")
                at(7 + c, quant_slip, 1, c, g)
        for i in range(4):
            at(12 + i // 2, p_piece, 0, 1, i)
            at(12 + (i + 1) // 2, q_piece, 0, 1, i)
            for s in range(2):
                at(13 + i, mm2, 0, i, s)
                at(14 + i, drain, 0, i, s, A_DRAIN[i, s])
        for k in range(4):
            at(18 + k, interleave, 0, k, "v")
            at(20 + k, quant_out, 0, k)
        at(21, store_words, 0, 0)
        at(23, store_words, 0, 1)
        at(23, store_scales, 0)
        for i in range(4):
            at((16, 17, 18, 19)[i], p_piece, 1, 0, i)
            at((17, 18, 19, 20)[i], q_piece, 1, 0, i)
        at(20, p_piece, 1, 1, 0)
        at(21, q_piece, 1, 1, 0)
        at(21, p_piece, 1, 1, 1)
        at(22, q_piece, 1, 1, 1)
        for i in range(2):
            for s in range(2):
                at(23, mm2, 1, i, s)

        turn(0, 0, 0)
        turn(0, 0, 1)
        turn_copy(0, 0, 0, "v")
        turn_copy(0, 0, 1, "s")
        permute("n", 0)
        quant_slip(0, 0, 0)
        quant_slip(0, 0, 1)
        permute("t", 0)
        permute_s(0)
        finish_l()
        last = len(units) - 1
        mm(0)
        for i in range(LEAD):
            mm(i + 1)
            x_step(i)
            r_step(i)
        for fn, args in aux.get(-1, []):
            fn(*args)
        for i in range(last + 1):
            if i + LEAD + 1 <= last:
                mm(i + LEAD + 1)
            if i + LEAD <= last:
                x_step(i + LEAD)
                r_step(i + LEAD)
            e_step(i)
            for fn, args in aux.get(i, []):
                fn(*args)

        p_piece(1, 1, 2)
        p_piece(1, 1, 3)
        q_piece(1, 1, 2)
        q_piece(1, 1, 3)
        for i in range(2):
            for s in range(2):
                drain(1, i, s, B_DRAIN[i, s])
        for s in range(2):
            for i in range(2, 4):
                mm2(1, i, s, "sn" if i == 2 else "st")
        for s in range(2):
            for i in range(2, 4):
                drain(1, i, s, B_DRAIN[i, s])
            interleave(1, 2 * s, "v")
            interleave(1, 2 * s + 1, "v")
            quant_out(1, 2 * s)
            quant_out(1, 2 * s + 1)
            store_words(1, s)
        store_scales(1)
